import numpy as np
import ml_dtypes

BF16 = ml_dtypes.bfloat16


def bf(x):
    return np.asarray(x, np.float32).astype(BF16)


def f32(x):
    return np.asarray(x, np.float32)


def f64(x):
    return np.asarray(x).astype(np.float64)


def striped(idx):
    return np.tile(idx.reshape(-1, 16).T, (8, 1))


S, K, M, N, B, Q = 512, 256, 128, 512, 4, 128


def setup_inputs():
    return {"base": bf(np.random.standard_normal((B, M, S))), "x": bf(np.random.standard_normal((K, N))), "w": bf(np.random.standard_normal((K, M)) / np.sqrt(K)), "b": f32(0.5 * np.random.standard_normal((M, 1))), "offs": striped(np.random.permutation(S))}


def reference(base, x, w, b, offs):
    idx = offs[:16].T.reshape(-1)
    z = f64(base).copy()
    for i in range(B):
        z[i][:, idx[i * Q : (i + 1) * Q]] += f64(w).T @ f64(x)[:, i * Q : (i + 1) * Q]
    return np.maximum(z + f64(b), 0.0)

@@ -1,0 +1,58 @@
+import concourse.mybir as mybir
+from concourse.masks import make_identity
+
+BF16, F32, U16 = mybir.dt.bfloat16, mybir.dt.float32, mybir.dt.uint16
+ADD, MAX = mybir.AluOpType.add, mybir.AluOpType.max
+RELU = mybir.ActivationFunctionType.Relu
+
+P = 128
+SEQUENCES, TOKENS = 4, 512
+BLOCKS = 2
+PIECE = 128
+PIECE_COLUMNS = PIECE // 16
+
+FLOPS = 2 * BLOCKS * P * P * SEQUENCES * PIECE + 3 * SEQUENCES * P * TOKENS
+
+
+def tile_scatter_matmul_kernel(tc, base, x, w, b, offs, out):
+    nc = tc.nc
+    with (
+        tc.tile_pool(name="held", bufs=1) as held,
+        tc.psum_pool(name="psum", bufs=1) as psum,
+    ):
+        base_tile = held.tile([P, SEQUENCES, TOKENS], BF16)
+        x_tile = held.tile([P, BLOCKS, SEQUENCES * PIECE], BF16)
+        w_tile = held.tile([P, BLOCKS, P], BF16)
+        offsets = held.tile([P, SEQUENCES * PIECE_COLUMNS], U16)
+        bias = held.tile([P, 1], F32)
+        nc.sync.dma_start(base_tile[:], base.rearrange("i p t -> p i t"))
+        nc.sync.dma_start(x_tile[:], x.rearrange("(p c) n -> p c n", c=BLOCKS))
+        nc.sync.dma_start(w_tile[:], w.rearrange("(p c) m -> p c m", c=BLOCKS))
+        nc.sync.dma_start(offsets[:], offs)
+        nc.sync.dma_start(bias[:], b)
+
+        identity = held.tile([P, P], BF16)
+        make_identity(nc, identity[:])
+
+        windows = [psum.tile([P, TOKENS], F32, name=f"window{i}") for i in range(SEQUENCES)]
+        for i in range(SEQUENCES):
+            nc.tensor.matmul(windows[i][:], identity[:], base_tile[:, i, :], start=True, stop=False)
+
+        for i in range(SEQUENCES):
+            places = offsets[:, i * PIECE_COLUMNS : (i + 1) * PIECE_COLUMNS]
+            for c in range(BLOCKS):
+                nc.tensor.matmul(
+                    windows[i][:].indirect(places),
+                    w_tile[:, c, :],
+                    x_tile[:, c, i * PIECE : (i + 1) * PIECE],
+                    start=False,
+                    stop=(c == BLOCKS - 1),
+                )
+
+        for i in range(SEQUENCES):
+            result = held.tile([P, TOKENS], F32, name=f"result{i}")
+            if i % 2 == 0:
+                nc.scalar.activation(result[:], windows[i][:], RELU, bias=bias[:])
+            else:
+                nc.vector.tensor_scalar(result[:], windows[i][:], bias[:], 0.0, ADD, MAX)
+            nc.sync.dma_start(out[i], result[:])

@@ -10,6 +10,7 @@ SEQUENCES, TOKENS = 4, 512
 BLOCKS = 2
 PIECE = 128
 PIECE_COLUMNS = PIECE // 16
+WARM_UPS = 5
 
 FLOPS = 2 * BLOCKS * P * P * SEQUENCES * PIECE + 3 * SEQUENCES * P * TOKENS
 
@@ -25,11 +26,20 @@ def tile_scatter_matmul_kernel(tc, base, x, w, b, offs, out):
         w_tile = held.tile([P, BLOCKS, P], BF16)
         offsets = held.tile([P, SEQUENCES * PIECE_COLUMNS], U16)
         bias = held.tile([P, 1], F32)
-        nc.sync.dma_start(base_tile[:], base.rearrange("i p t -> p i t"))
+        for i in range(SEQUENCES):
+            nc.sync.dma_start(base_tile[:, i, :], base[i])
         nc.sync.dma_start(x_tile[:], x.rearrange("(p c) n -> p c n", c=BLOCKS))
         nc.sync.dma_start(w_tile[:], w.rearrange("(p c) m -> p c m", c=BLOCKS))
         nc.sync.dma_start(offsets[:], offs)
         nc.sync.dma_start(bias[:], b)
+
+        zeros = held.tile([P, TOKENS], BF16)
+        nc.vector.memset(zeros[:], 0.0)
+        spare = psum.tile([P, TOKENS], F32)
+        for turn in range(WARM_UPS):
+            nc.tensor.matmul(spare[:], zeros[:, 0:P], zeros[:], start=True, stop=True)
+        first_relu = held.tile([P, 1], F32)
+        nc.scalar.activation(first_relu[:], zeros[:, 0:1], RELU)
 
         identity = held.tile([P, P], BF16)
         make_identity(nc, identity[:])

@@ -10,7 +10,7 @@ SEQUENCES, TOKENS = 4, 512
 BLOCKS = 2
 PIECE = 128
 PIECE_COLUMNS = PIECE // 16
-WARM_UPS = 5
+WARM_UPS = 3
 
 FLOPS = 2 * BLOCKS * P * P * SEQUENCES * PIECE + 3 * SEQUENCES * P * TOKENS
 
@@ -60,9 +60,11 @@ def tile_scatter_matmul_kernel(tc, base, x, w, b, offs, out):
                 )
 
         for i in range(SEQUENCES):
-            result = held.tile([P, TOKENS], F32, name=f"result{i}")
-            if i % 2 == 0:
-                nc.scalar.activation(result[:], windows[i][:], RELU, bias=bias[:])
-            else:
-                nc.vector.tensor_scalar(result[:], windows[i][:], bias[:], 0.0, ADD, MAX)
-            nc.sync.dma_start(out[i], result[:])
+            for h in range(2):
+                half = slice(h * (TOKENS // 2), (h + 1) * (TOKENS // 2))
+                result = held.tile([P, TOKENS // 2], F32, name=f"result{i}_{h}")
+                if i % 2 == 0:
+                    nc.scalar.activation(result[:], windows[i][:, half], RELU, bias=bias[:])
+                else:
+                    nc.vector.tensor_scalar(result[:], windows[i][:, half], bias[:], 0.0, ADD, MAX)
+                nc.sync.dma_start(out[i][:, half], result[:])

@@ -26,11 +26,13 @@ def tile_scatter_matmul_kernel(tc, base, x, w, b, offs, out):
         w_tile = held.tile([P, BLOCKS, P], BF16)
         offsets = held.tile([P, SEQUENCES * PIECE_COLUMNS], U16)
         bias = held.tile([P, 1], F32)
-        for i in range(SEQUENCES):
-            nc.sync.dma_start(base_tile[:, i, :], base[i])
-        nc.sync.dma_start(x_tile[:], x.rearrange("(p c) n -> p c n", c=BLOCKS))
+        for pair in (slice(0, 2), slice(2, 4)):
+            nc.sync.dma_start(base_tile[:, pair, :], base[pair].rearrange("i p t -> p i t"))
         nc.sync.dma_start(w_tile[:], w.rearrange("(p c) m -> p c m", c=BLOCKS))
         nc.sync.dma_start(offsets[:], offs)
+        x_rows = x.rearrange("(p c) n -> p c n", c=BLOCKS)
+        for entries in (slice(0, 2 * PIECE), slice(2 * PIECE, 4 * PIECE)):
+            nc.sync.dma_start(x_tile[:, :, entries], x_rows[:, :, entries])
         nc.sync.dma_start(bias[:], b)
 
         zeros = held.tile([P, TOKENS], BF16)
@@ -64,7 +66,7 @@ def tile_scatter_matmul_kernel(tc, base, x, w, b, offs, out):
                 half = slice(h * (TOKENS // 2), (h + 1) * (TOKENS // 2))
                 result = held.tile([P, TOKENS // 2], F32, name=f"result{i}_{h}")
                 if i % 2 == 0:
-                    nc.scalar.activation(result[:], windows[i][:, half], RELU, bias=bias[:])
-                else:
                     nc.vector.tensor_scalar(result[:], windows[i][:, half], bias[:], 0.0, ADD, MAX)
+                else:
+                    nc.scalar.activation(result[:], windows[i][:, half], RELU, bias=bias[:])
                 nc.sync.dma_start(out[i][:, half], result[:])

import concourse.mybir as mybir
from concourse.masks import make_identity

BF16, F32, U16 = mybir.dt.bfloat16, mybir.dt.float32, mybir.dt.uint16
ADD, MAX = mybir.AluOpType.add, mybir.AluOpType.max
RELU = mybir.ActivationFunctionType.Relu

P = 128
SEQUENCES, TOKENS = 4, 512
BLOCKS = 2
PIECE = 128
PIECE_COLUMNS = PIECE // 16
WARM_UPS = 3

FLOPS = 2 * BLOCKS * P * P * SEQUENCES * PIECE + 3 * SEQUENCES * P * TOKENS


def tile_scatter_matmul_kernel(tc, base, x, w, b, offs, out):
    nc = tc.nc
    with (
        tc.tile_pool(name="held", bufs=1) as held,
        tc.psum_pool(name="psum", bufs=1) as psum,
    ):
        base_tile = held.tile([P, SEQUENCES, TOKENS], BF16)
        x_tile = held.tile([P, BLOCKS, SEQUENCES * PIECE], BF16)
        w_tile = held.tile([P, BLOCKS, P], BF16)
        offsets = held.tile([P, SEQUENCES * PIECE_COLUMNS], U16)
        bias = held.tile([P, 1], F32)
        for pair in (slice(0, 2), slice(2, 4)):
            nc.sync.dma_start(base_tile[:, pair, :], base[pair].rearrange("i p t -> p i t"))
        nc.sync.dma_start(w_tile[:], w.rearrange("(p c) m -> p c m", c=BLOCKS))
        nc.sync.dma_start(offsets[:], offs)
        x_rows = x.rearrange("(p c) n -> p c n", c=BLOCKS)
        for entries in (slice(0, 2 * PIECE), slice(2 * PIECE, 4 * PIECE)):
            nc.sync.dma_start(x_tile[:, :, entries], x_rows[:, :, entries])
        nc.sync.dma_start(bias[:], b)

        zeros = held.tile([P, TOKENS], BF16)
        nc.vector.memset(zeros[:], 0.0)
        spare = psum.tile([P, TOKENS], F32)
        for turn in range(WARM_UPS):
            nc.tensor.matmul(spare[:], zeros[:, 0:P], zeros[:], start=True, stop=True)
        first_relu = held.tile([P, 1], F32)
        nc.scalar.activation(first_relu[:], zeros[:, 0:1], RELU)

        identity = held.tile([P, P], BF16)
        make_identity(nc, identity[:])

        windows = [psum.tile([P, TOKENS], F32, name=f"window{i}") for i in range(SEQUENCES)]
        for i in range(SEQUENCES):
            nc.tensor.matmul(windows[i][:], identity[:], base_tile[:, i, :], start=True, stop=False)

        for i in range(SEQUENCES):
            places = offsets[:, i * PIECE_COLUMNS : (i + 1) * PIECE_COLUMNS]
            for c in range(BLOCKS):
                nc.tensor.matmul(
                    windows[i][:].indirect(places),
                    w_tile[:, c, :],
                    x_tile[:, c, i * PIECE : (i + 1) * PIECE],
                    start=False,
                    stop=(c == BLOCKS - 1),
                )

        for i in range(SEQUENCES):
            for h in range(2):
                half = slice(h * (TOKENS // 2), (h + 1) * (TOKENS // 2))
                result = held.tile([P, TOKENS // 2], F32, name=f"result{i}_{h}")
                if i % 2 == 0:
                    nc.vector.tensor_scalar(result[:], windows[i][:, half], bias[:], 0.0, ADD, MAX)
                else:
                    nc.scalar.activation(result[:], windows[i][:, half], RELU, bias=bias[:])
                nc.sync.dma_start(out[i][:, half], result[:])
